import numpy as np
import ml_dtypes


def mxq(x, axis, fmt="e4m3"):
    dtype, down = {"e4m3": (ml_dtypes.float8_e4m3fn, 7), "e5m2": (ml_dtypes.float8_e5m2, 14)}[fmt]
    v = np.moveaxis(np.asarray(x, np.float32).astype(ml_dtypes.bfloat16).astype(np.float64), axis, -1)
    blocks = v.reshape(v.shape[:-1] + (-1, 32))
    amax = np.abs(blocks).max(-1, keepdims=True)
    byte = np.maximum(np.where(amax > 0, np.frexp(amax)[1] - 1 + 127, 0) - down, 1)
    scale = np.exp2(byte - 127.0)
    codes = (blocks / scale).astype(np.float32).astype(dtype).astype(np.float64)
    return np.moveaxis((codes * scale).reshape(v.shape), -1, axis)


WIDE = False


def mx_kscale(k):
    if not WIDE:
        return np.ones(k)
    levels = np.array([10, -10, 5, -5, 0])
    if k % 512:
        return np.exp2(np.random.permutation(np.resize(levels, k // 32))).repeat(32)
    a = np.empty((k // 512, 16))
    for p in range(k // 512):
        a[p, :8] = np.random.permutation(np.resize(levels, 8))
        for g in range(8):
            far = levels[np.abs(levels - a[p, g]) >= 10]
            a[p, g + 8] = far[np.random.randint(len(far))]
    return np.exp2(a.ravel()).repeat(32)


def f64(x):
    return np.asarray(x).astype(np.float64)


def striped(idx):
    return np.tile(np.asarray(idx).reshape(-1, 16).T, (8, 1)).astype(np.uint16)


def unstriped(offs):
    return offs[:16].T.reshape(-1).astype(np.int64)


def striped8(idx):
    return np.asarray(idx).reshape(8, -1, 16).transpose(0, 2, 1).reshape(128, -1).astype(np.uint16)


def unstriped8(offs):
    return offs.reshape(8, 16, -1).transpose(0, 2, 1).reshape(8, -1).astype(np.int64)


def pick8(x, idx, run):
    r = np.arange(len(x))
    return x[r[:, None], idx[r % (8 * run) // run]]


E2M1 = np.array([0.0, 0.5, 1.0, 1.5, 2.0, 3.0, 4.0, 6.0, -0.0, -0.5, -1.0, -1.5, -2.0, -3.0, -4.0, -6.0])


def pack_weight(w, fmt):
    k, n = w.shape
    w = f64(np.asarray(w, np.float32).astype(ml_dtypes.bfloat16)).reshape(k // 32, 32, n)
    amax = np.abs(w).max(1)
    if fmt == "e4m3":
        byte = np.frexp(amax)[1] - 1 + 127 - 7
    else:
        mant, ex = np.frexp(amax / 6.0)
        byte = np.where(mant > 0.5, ex, ex - 1) + 127
    byte = np.clip(np.where(amax > 0, byte, 1), 1, 254)
    scaled = (w * np.exp2(127.0 - byte)[:, None, :]).reshape(k, n).astype(np.float32)
    by_word = np.ascontiguousarray(scaled.reshape(k // 512, 128, 4, n).transpose(0, 1, 3, 2))
    if fmt == "e4m3":
        words = by_word.astype(ml_dtypes.float8_e4m3fn).view(np.uint8)
    else:
        c = by_word.astype(ml_dtypes.float4_e2m1fn).view(np.uint8) & 0xF
        words = (c[..., 0::2] | (c[..., 1::2] << 4)).reshape(k // 512, 128, 2 * n)
    return np.ascontiguousarray(words), np.ascontiguousarray(byte.astype(np.uint8).reshape(k // 512, 16, n))


def unpack_weight(words, scales, fmt):
    g, _, n = scales.shape
    words = np.ascontiguousarray(words).reshape(g, 128, n, -1)
    if fmt == "e4m3":
        vals = words.view(ml_dtypes.float8_e4m3fn).astype(np.float64)
    else:
        nib = np.empty((g, 128, n, 4), np.uint8)
        nib[..., 0::2] = words & 0xF
        nib[..., 1::2] = words >> 4
        vals = E2M1[nib]
    vals = vals * np.repeat(np.exp2(scales.astype(np.float64) - 127.0), 8, axis=1)[..., None]
    return vals.transpose(0, 1, 3, 2).reshape(g * 512, n)


K, R, F, T, J, U = 512, 128, 512, 2048, 512, 1024


def setup_inputs():
    n = np.random.standard_normal
    idx = np.random.permutation(T)[:J]
    idx2 = np.stack([np.random.permutation(U)[:J] for _ in range(8)])
    idx3 = np.stack([np.random.permutation(U)[:J] for _ in range(8)])
    fk = mx_kscale(K)
    dtabp = pack_weight(n((K, T)) / fk[:, None], "e2m1")
    tabp = pack_weight(n((K, T)) / fk[:, None], "e2m1")
    return {
        "dtab_words": dtabp[0],
        "dtab_scales": dtabp[1],
        "tab_words": tabp[0],
        "tab_scales": tabp[1],
        "w1": (n((K, R)) * 1 / np.sqrt(K) * fk[:, None]).astype(np.float32),
        "gain": (np.random.uniform(0.5, 1.5, (R, 1))).astype(np.float32),
        "ground": (n((R, U)) * 0.7).astype(np.float32),
        "og": (np.random.uniform(0.5, 2.0, (R, 1))).astype(np.float32),
        "base": (0.3 * n((R, U))).astype(np.float32),
        "offs": striped(idx),
        "offs2": striped8(idx2),
        "offs3": striped8(idx3),
    }


def reference(dtab_words, dtab_scales, tab_words, tab_scales, w1, gain, ground, og, base, offs, offs2, offs3):
    idx = unstriped(offs)
    idx2 = unstriped8(offs2)
    idx3 = unstriped8(offs3)
    dtabu = unpack_weight(dtab_words, dtab_scales, "e2m1")
    tabu = unpack_weight(tab_words, tab_scales, "e2m1")
    w1q = mxq(f64(w1), 0, "e4m3")
    tabidxg = tabu[:, idx]
    a = w1q.T @ tabidxg
    dtabidxg = dtabu[:, idx]
    ta = w1q.T @ dtabidxg
    h1 = a * f64(gain)
    pa = np.zeros((R, U))
    pa[np.arange(R)[:, None], idx2[np.arange(R) % 128 // 16]] = h1
    pb = np.zeros((R, U))
    pb[np.arange(R)[:, None], idx3[np.arange(R) % 128 // 16]] = a
    th1 = ta * f64(gain)
    tpa = np.zeros((R, U))
    tpa[np.arange(R)[:, None], idx2[np.arange(R) % 128 // 16]] = th1
    tpb = np.zeros((R, U))
    tpb[np.arange(R)[:, None], idx3[np.arange(R) % 128 // 16]] = ta
    tu1 = tpa * (1.0 - np.square(np.tanh(pa + f64(ground)))) * (pb + f64(ground)) + tpb * np.tanh(pa + f64(ground))
    y = tu1 * f64(og) + f64(base)
    return y

@@ -1,0 +1,162 @@
+from contextlib import ExitStack
+
+import concourse.mybir as mybir
+
+K, R, T, J, U = 512, 128, 2048, 512, 1024
+FLOPS = 2 * 2 * K * R * J
+
+F32 = mybir.dt.float32
+BF16 = mybir.dt.bfloat16
+I32 = mybir.dt.int32
+U32 = mybir.dt.uint32
+U16 = mybir.dt.uint16
+U8 = mybir.dt.uint8
+FP8X4 = mybir.dt.float8_e4m3fn_x4
+FP4X4 = mybir.dt.float4_e2m1fn_x4
+ACT = mybir.ActivationFunctionType
+ALU = mybir.AluOpType
+
+P = 128
+HALF = J // 2
+CH = 256
+
+
+def tile_attend_ttwopages_kernel(tc, dtab_words, dtab_scales, tab_words, tab_scales, w1, gain, ground, og, base,
+                                  offs, offs2, offs3, out):
+    nc = tc.nc
+    with ExitStack() as ctx:
+        lists = ctx.enter_context(tc.tile_pool(name="lists", bufs=1))
+        sb = ctx.enter_context(tc.tile_pool(name="sb", bufs=1))
+        psum = ctx.enter_context(tc.psum_pool(name="psum", bufs=1))
+
+        pick = lists.tile([P, J // 16], U16, name="pick")
+        page_a = lists.tile([P, J // 16], U16, name="page_a")
+        page_b = lists.tile([P, J // 16], U16, name="page_b")
+
+        tab_s = sb.tile([P, T], U8, name="tab_s", tag="tab_s", align_bytes=64)
+        dtab_s = sb.tile([P, T], U8, name="dtab_s", align_bytes=64)
+        nc.vector.memset(tab_s[:].bitcast(I32), 0)
+        nc.vector.memset(dtab_s[:].bitcast(I32), 0)
+
+        def load_scales(queue, tile, scales):
+            for q in range(4):
+                queue.dma_start(out=tile[32 * q:32 * q + 4, :].bitcast(I32),
+                                    in_=scales[0, 4 * q:4 * q + 4, :].bitcast(I32))
+
+        nc.sync.dma_start(pick[:], offs)
+        nc.sync.dma_start(page_a[:], offs2)
+        nc.sync.dma_start(page_b[:], offs3)
+        tab_w = sb.tile([P, T], U16, name="tab_w", tag="tab_w", align_bytes=64)
+        nc.sync.dma_start(out=tab_w[:].bitcast(I32), in_=tab_words[0].bitcast(I32))
+        load_scales(nc.scalar, tab_s, tab_scales)
+        w_raw = sb.tile([P, 4, R], F32, name="w_raw")
+        nc.sync.dma_start(out=w_raw[:], in_=w1.rearrange("(p t) r -> p t r", t=4))
+        dtab_w = sb.tile([P, T], U16, name="dtab_w", align_bytes=64)
+        nc.sync.dma_start(out=dtab_w[:].bitcast(I32), in_=dtab_words[0].bitcast(I32))
+        load_scales(nc.sync, dtab_s, dtab_scales)
+        gain_c = sb.tile([P, 1], F32, name="gain_c")
+        og_c = sb.tile([P, 1], F32, name="og_c")
+        nc.gpsimd.dma_start(out=gain_c[:], in_=gain)
+        nc.gpsimd.dma_start(out=og_c[:], in_=og)
+
+        pa = sb.tile([P, U], F32, name="pa")
+        pb = sb.tile([P, U], F32, name="pb")
+        tpa = sb.tile([P, U], F32, name="tpa")
+        tpb = sb.tile([P, U], F32, name="tpb")
+        for page in (pa, pb, tpb, tpa):
+            nc.vector.memset(page[:], 0.0)
+
+        w_bf = sb.tile([P, R, 4], BF16, name="w_bf", align_bytes=64)
+        nc.scalar.copy(out=w_bf[:], in_=w_raw[:].rearrange("p t r -> p r t"))
+        w_codes = sb.tile([P, R], U32, name="w_codes", align_bytes=64)
+        w_scales = sb.tile([P, R], U8, name="w_scales", align_bytes=64)
+
+        tab_gw = sb.tile([P, J], U16, name="tab_gw", align_bytes=64)
+        tab_gs = sb.tile([P, J], U8, name="tab_gs", align_bytes=64)
+        nc.vector.tensor_copy(tab_gw[:], tab_w[:].indirect(pick[:]))
+        nc.vector.quantize_mx(out=w_codes[:].bitcast(FP8X4), scales=w_scales[:],
+                              in_=w_bf[:].rearrange("p r t -> p (r t)"))
+        nc.vector.tensor_copy(tab_gs[:], tab_s[:].indirect(pick[:]))
+
+        ground_sb = sb.tile([P, U], F32, name="ground_sb", tag="tab_w", align_bytes=64)
+        nc.sync.dma_start(out=ground_sb[:], in_=ground)
+        base_sb = sb.tile([P, U], F32, name="base_sb", tag="tab_s", align_bytes=64)
+        nc.sync.dma_start(out=base_sb[:], in_=base)
+
+        gain_og = sb.tile([P, 1], F32, name="gain_og")
+        nc.scalar.activation(gain_og[:], gain_c[:], ACT.Copy, scale=og_c[:])
+
+        a_ps = psum.tile([P, J], F32, name="a_ps")
+        nc.tensor.matmul_mx(out=a_ps[:], lhsT=w_codes[:].bitcast(FP8X4), lhsT_scale=w_scales[:],
+                            rhs=tab_gw[:].bitcast(FP4X4), rhs_scale=tab_gs[:], start=True, stop=True)
+        h1 = sb.tile([P, J], F32, name="h1", tag="h1", align_bytes=64)
+        a_sb = sb.tile([P, J], F32, name="a_sb", tag="a_sb", align_bytes=64)
+        nc.scalar.activation(h1[:], a_ps[:], ACT.Copy, scale=gain_c[:])
+        nc.scalar.copy(out=a_sb[:], in_=a_ps[:])
+
+        ta_og = [sb.tile([P, HALF], F32, name=f"ta_og{h}") for h in range(2)]
+        th1_og = sb.tile([P, J], F32, name="th1_og")
+
+        def tangent_half(h, tag_w, tag_s):
+            cols = slice(h * HALF // 16, (h + 1) * HALF // 16)
+            gw = sb.tile([P, HALF], U16, name=f"dtab_gw{h}", tag=tag_w, align_bytes=64)
+            gs = sb.tile([P, HALF], U8, name=f"dtab_gs{h}", tag=tag_s, align_bytes=64)
+            nc.vector.tensor_copy(gw[:], dtab_w[:].indirect(pick[:, cols]))
+            nc.vector.tensor_copy(gs[:], dtab_s[:].indirect(pick[:, cols]))
+            ta_ps = psum.tile([P, HALF], F32, name=f"ta_ps{h}")
+            nc.tensor.matmul_mx(out=ta_ps[:], lhsT=w_codes[:].bitcast(FP8X4), lhsT_scale=w_scales[:],
+                                rhs=gw[:].bitcast(FP4X4), rhs_scale=gs[:], start=True, stop=True)
+            nc.scalar.activation(ta_og[h][:], ta_ps[:], ACT.Copy, scale=og_c[:])
+            nc.scalar.activation(th1_og[:, h * HALF:(h + 1) * HALF], ta_ps[:], ACT.Copy, scale=gain_og[:])
+
+        tangent_half(0, "dtab_gw0", "dtab_gs0")
+        nc.vector.tensor_copy(pa[:].indirect(page_a[:]), h1[:])
+        nc.vector.tensor_copy(pb[:].indirect(page_b[:]), a_sb[:])
+
+        th = sb.tile([P, U], F32, name="th")
+        slope = sb.tile([P, U], F32, name="slope")
+        for h in range(2):
+            cols = slice(h * J, (h + 1) * J)
+            arg = sb.tile([P, J], F32, name=f"arg{h}")
+            sq = sb.tile([P, J], F32, name=f"sq{h}")
+            nc.gpsimd.tensor_tensor(arg[:], pa[:, cols], ground_sb[:, cols], ALU.add)
+            nc.scalar.activation(th[:, cols], arg[:], ACT.Tanh)
+            nc.scalar.activation(sq[:], th[:, cols], ACT.Square)
+            nc.scalar.activation(slope[:, cols], sq[:], ACT.Copy, scale=-1.0, bias=1.0)
+
+        tangent_half(1, "h1", "a_sb")
+
+        coef = sb.tile([P, U], F32, name="coef")
+        for h in range(2):
+            cols = slice(h * J, (h + 1) * J)
+            second = sb.tile([P, J], F32, name=f"second{h}")
+            nc.gpsimd.tensor_tensor(second[:], pb[:, cols], ground_sb[:, cols], ALU.add)
+            nc.gpsimd.tensor_tensor(coef[:, cols], second[:], slope[:, cols], ALU.mult)
+
+        for h in range(2):
+            nc.vector.tensor_copy(tpb[:].indirect(page_b[:, h * HALF // 16:(h + 1) * HALF // 16]), ta_og[h][:])
+        nc.vector.tensor_copy(tpa[:].indirect(page_a[:]), th1_og[:])
+
+        chunks = [slice(c * CH, (c + 1) * CH) for c in range(U // CH)]
+        rest = [sb.tile([P, CH], F32, name=f"rest{c}") for c in range(len(chunks))]
+        for c, cols in enumerate(chunks):
+            term = sb.tile([P, CH], F32, name=f"term{c}")
+            if c < 2:
+                nc.gpsimd.tensor_tensor(term[:], tpb[:, cols], th[:, cols], ALU.mult)
+                nc.gpsimd.tensor_tensor(rest[c][:], term[:], base_sb[:, cols], ALU.add)
+            else:
+                nc.gpsimd.tensor_tensor(rest[c][:], tpb[:, cols], th[:, cols], ALU.mult)
+
+        lead = [sb.tile([P, CH], F32, name=f"lead{c}") for c in range(len(chunks))]
+        res = [sb.tile([P, CH], F32, name=f"res{c}") for c in range(len(chunks))]
+        for pair in ((0, 1), (2, 3)):
+            for c in pair:
+                nc.vector.tensor_tensor(lead[c][:], tpa[:, chunks[c]], coef[:, chunks[c]], ALU.mult)
+            for c in pair:
+                if c >= 2:
+                    mid = sb.tile([P, CH], F32, name=f"mid{c}")
+                    nc.vector.tensor_tensor(mid[:], lead[c][:], base_sb[:, chunks[c]], ALU.add)
+                    lead[c] = mid
+            for c in pair:
+                nc.vector.tensor_tensor(res[c][:], lead[c][:], rest[c][:], ALU.add)
+                nc.sync.dma_start(out=out[:, chunks[c]], in_=res[c][:])

@@ -1,6 +1,7 @@
 from contextlib import ExitStack
 
 import concourse.mybir as mybir
+from concourse.masks import make_identity
 
 K, R, T, J, U = 512, 128, 2048, 512, 1024
 FLOPS = 2 * 2 * K * R * J
@@ -27,6 +28,7 @@ def tile_attend_ttwopages_kernel(tc, dtab_words, dtab_scales, tab_words, tab_sca
     with ExitStack() as ctx:
         lists = ctx.enter_context(tc.tile_pool(name="lists", bufs=1))
         sb = ctx.enter_context(tc.tile_pool(name="sb", bufs=1))
+        reuse = ctx.enter_context(tc.tile_pool(name="reuse", bufs=1))
         psum = ctx.enter_context(tc.psum_pool(name="psum", bufs=1))
 
         pick = lists.tile([P, J // 16], U16, name="pick")
@@ -34,7 +36,7 @@ def tile_attend_ttwopages_kernel(tc, dtab_words, dtab_scales, tab_words, tab_sca
         page_b = lists.tile([P, J // 16], U16, name="page_b")
 
         tab_s = sb.tile([P, T], U8, name="tab_s", tag="tab_s", align_bytes=64)
-        dtab_s = sb.tile([P, T], U8, name="dtab_s", align_bytes=64)
+        dtab_s = sb.tile([P, T], U8, name="dtab_s", tag="dtab_s", align_bytes=64)
         nc.vector.memset(tab_s[:].bitcast(I32), 0)
         nc.vector.memset(dtab_s[:].bitcast(I32), 0)
 
@@ -44,28 +46,31 @@ def tile_attend_ttwopages_kernel(tc, dtab_words, dtab_scales, tab_words, tab_sca
                                     in_=scales[0, 4 * q:4 * q + 4, :].bitcast(I32))
 
         nc.sync.dma_start(pick[:], offs)
-        nc.sync.dma_start(page_a[:], offs2)
-        nc.sync.dma_start(page_b[:], offs3)
         tab_w = sb.tile([P, T], U16, name="tab_w", tag="tab_w", align_bytes=64)
         nc.sync.dma_start(out=tab_w[:].bitcast(I32), in_=tab_words[0].bitcast(I32))
+        nc.sync.dma_start(page_a[:], offs2)
+        nc.sync.dma_start(page_b[:], offs3)
         load_scales(nc.scalar, tab_s, tab_scales)
         w_raw = sb.tile([P, 4, R], F32, name="w_raw")
         nc.sync.dma_start(out=w_raw[:], in_=w1.rearrange("(p t) r -> p t r", t=4))
-        dtab_w = sb.tile([P, T], U16, name="dtab_w", align_bytes=64)
+        dtab_w = sb.tile([P, T], U16, name="dtab_w", tag="dtab_w", align_bytes=64)
         nc.sync.dma_start(out=dtab_w[:].bitcast(I32), in_=dtab_words[0].bitcast(I32))
         load_scales(nc.sync, dtab_s, dtab_scales)
-        gain_c = sb.tile([P, 1], F32, name="gain_c")
+        gain_c = sb.tile([P, 1], F32, name="gain_c", tag="a_sb", align_bytes=64)
         og_c = sb.tile([P, 1], F32, name="og_c")
         nc.gpsimd.dma_start(out=gain_c[:], in_=gain)
         nc.gpsimd.dma_start(out=og_c[:], in_=og)
 
-        pa = sb.tile([P, U], F32, name="pa")
         pb = sb.tile([P, U], F32, name="pb")
         tpa = sb.tile([P, U], F32, name="tpa")
         tpb = sb.tile([P, U], F32, name="tpb")
-        for page in (pa, pb, tpb, tpa):
+        for page in (pb, tpb, tpa):
             nc.vector.memset(page[:], 0.0)
 
+        ident = sb.tile([P, P], F32, name="ident")
+        make_identity(nc, ident[:])
+        warm = sb.tile([P, 1], F32, name="warm")
+        nc.scalar.activation(warm[:], pb[:, 0:1], ACT.Tanh)
         w_bf = sb.tile([P, R, 4], BF16, name="w_bf", align_bytes=64)
         nc.scalar.copy(out=w_bf[:], in_=w_raw[:].rearrange("p t r -> p r t"))
         w_codes = sb.tile([P, R], U32, name="w_codes", align_bytes=64)
@@ -86,30 +91,18 @@ def tile_attend_ttwopages_kernel(tc, dtab_words, dtab_scales, tab_words, tab_sca
         gain_og = sb.tile([P, 1], F32, name="gain_og")
         nc.scalar.activation(gain_og[:], gain_c[:], ACT.Copy, scale=og_c[:])
 
-        a_ps = psum.tile([P, J], F32, name="a_ps")
+        a_ps = psum.tile([P, J], F32, name="a_ps", tag="a_ps")
         nc.tensor.matmul_mx(out=a_ps[:], lhsT=w_codes[:].bitcast(FP8X4), lhsT_scale=w_scales[:],
                             rhs=tab_gw[:].bitcast(FP4X4), rhs_scale=tab_gs[:], start=True, stop=True)
-        h1 = sb.tile([P, J], F32, name="h1", tag="h1", align_bytes=64)
+        h1 = reuse.tile([P, J], F32, name="h1", offset=0, align_bytes=64)
         a_sb = sb.tile([P, J], F32, name="a_sb", tag="a_sb", align_bytes=64)
         nc.scalar.activation(h1[:], a_ps[:], ACT.Copy, scale=gain_c[:])
         nc.scalar.copy(out=a_sb[:], in_=a_ps[:])
 
-        ta_og = [sb.tile([P, HALF], F32, name=f"ta_og{h}") for h in range(2)]
-        th1_og = sb.tile([P, J], F32, name="th1_og")
-
-        def tangent_half(h, tag_w, tag_s):
-            cols = slice(h * HALF // 16, (h + 1) * HALF // 16)
-            gw = sb.tile([P, HALF], U16, name=f"dtab_gw{h}", tag=tag_w, align_bytes=64)
-            gs = sb.tile([P, HALF], U8, name=f"dtab_gs{h}", tag=tag_s, align_bytes=64)
-            nc.vector.tensor_copy(gw[:], dtab_w[:].indirect(pick[:, cols]))
-            nc.vector.tensor_copy(gs[:], dtab_s[:].indirect(pick[:, cols]))
-            ta_ps = psum.tile([P, HALF], F32, name=f"ta_ps{h}")
-            nc.tensor.matmul_mx(out=ta_ps[:], lhsT=w_codes[:].bitcast(FP8X4), lhsT_scale=w_scales[:],
-                                rhs=gw[:].bitcast(FP4X4), rhs_scale=gs[:], start=True, stop=True)
-            nc.scalar.activation(ta_og[h][:], ta_ps[:], ACT.Copy, scale=og_c[:])
-            nc.scalar.activation(th1_og[:, h * HALF:(h + 1) * HALF], ta_ps[:], ACT.Copy, scale=gain_og[:])
-
-        tangent_half(0, "dtab_gw0", "dtab_gs0")
+        dtab_gw = sb.tile([P, J], U16, name="dtab_gw", align_bytes=64)
+        nc.vector.tensor_copy(dtab_gw[:], dtab_w[:].indirect(pick[:]))
+        pa = sb.tile([P, U], F32, name="pa", tag="dtab_w", align_bytes=64)
+        nc.vector.memset(pa[:], 0.0)
         nc.vector.tensor_copy(pa[:].indirect(page_a[:]), h1[:])
         nc.vector.tensor_copy(pb[:].indirect(page_b[:]), a_sb[:])
 
@@ -117,46 +110,74 @@ def tile_attend_ttwopages_kernel(tc, dtab_words, dtab_scales, tab_words, tab_sca
         slope = sb.tile([P, U], F32, name="slope")
         for h in range(2):
             cols = slice(h * J, (h + 1) * J)
-            arg = sb.tile([P, J], F32, name=f"arg{h}")
-            sq = sb.tile([P, J], F32, name=f"sq{h}")
+            arg = sb.tile([P, J], F32, name=f"arg{h}", tag=f"arg{h}")
+            sq = sb.tile([P, J], F32, name=f"sq{h}", tag=f"sq{h}")
             nc.gpsimd.tensor_tensor(arg[:], pa[:, cols], ground_sb[:, cols], ALU.add)
             nc.scalar.activation(th[:, cols], arg[:], ACT.Tanh)
             nc.scalar.activation(sq[:], th[:, cols], ACT.Square)
             nc.scalar.activation(slope[:, cols], sq[:], ACT.Copy, scale=-1.0, bias=1.0)
 
-        tangent_half(1, "h1", "a_sb")
+        ta_og = []
+        ta_ps = []
+        for h in range(2):
+            slots = slice(h * HALF, (h + 1) * HALF)
+            gs = reuse.tile([P, HALF], U8, name=f"dtab_gs{h}", offset=h * HALF, align_bytes=64)
+            nc.vector.tensor_copy(gs[:], dtab_s[:].indirect(pick[:, h * HALF // 16:(h + 1) * HALF // 16]))
+            ta_ps.append(psum.tile([P, HALF], F32, name=f"ta_ps{h}", tag=f"ta_ps{h}"))
+            nc.tensor.matmul_mx(out=ta_ps[h][:], lhsT=w_codes[:].bitcast(FP8X4), lhsT_scale=w_scales[:],
+                                rhs=dtab_gw[:, slots].bitcast(FP4X4), rhs_scale=gs[:], start=True, stop=True)
+            ta_og.append(arg[:, slots])
+            nc.scalar.activation(ta_og[h], ta_ps[h][:], ACT.Copy, scale=og_c[:])
+        th1_og = sq
+        for h in range(2):
+            nc.scalar.activation(th1_og[:, h * HALF:(h + 1) * HALF], ta_ps[h][:], ACT.Copy, scale=gain_og[:])
 
         coef = sb.tile([P, U], F32, name="coef")
         for h in range(2):
             cols = slice(h * J, (h + 1) * J)
-            second = sb.tile([P, J], F32, name=f"second{h}")
+            second = sb.tile([P, J], F32, name=f"second{h}", tag=f"second{h}")
             nc.gpsimd.tensor_tensor(second[:], pb[:, cols], ground_sb[:, cols], ALU.add)
             nc.gpsimd.tensor_tensor(coef[:, cols], second[:], slope[:, cols], ALU.mult)
 
         for h in range(2):
-            nc.vector.tensor_copy(tpb[:].indirect(page_b[:, h * HALF // 16:(h + 1) * HALF // 16]), ta_og[h][:])
+            nc.vector.tensor_copy(tpb[:].indirect(page_b[:, h * HALF // 16:(h + 1) * HALF // 16]), ta_og[h])
         nc.vector.tensor_copy(tpa[:].indirect(page_a[:]), th1_og[:])
 
         chunks = [slice(c * CH, (c + 1) * CH) for c in range(U // CH)]
-        rest = [sb.tile([P, CH], F32, name=f"rest{c}") for c in range(len(chunks))]
+        terms = [second[:, :CH], second[:, CH:], slope[:, J:J + CH], slope[:, J + CH:]]
+        rest = []
         for c, cols in enumerate(chunks):
-            term = sb.tile([P, CH], F32, name=f"term{c}")
-            if c < 2:
-                nc.gpsimd.tensor_tensor(term[:], tpb[:, cols], th[:, cols], ALU.mult)
-                nc.gpsimd.tensor_tensor(rest[c][:], term[:], base_sb[:, cols], ALU.add)
-            else:
-                nc.gpsimd.tensor_tensor(rest[c][:], tpb[:, cols], th[:, cols], ALU.mult)
+            nc.gpsimd.tensor_tensor(terms[c], tpb[:, cols], th[:, cols], ALU.mult)
+            if c == 3:
+                break
+            turned_ps = psum.tile([P, CH], F32, name=f"turned_ps{c}", tag="turned_ps", bufs=2)
+            for b in range(CH // P):
+                blk = slice(b * P, (b + 1) * P)
+                nc.tensor.matmul(turned_ps[:, blk], base_sb[:, c * CH + b * P:c * CH + (b + 1) * P], ident[:],
+                                 start=True, stop=False, is_transpose=True)
+                nc.tensor.matmul(turned_ps[:, blk], terms[c][:, blk], ident[:],
+                                 start=False, stop=True, is_transpose=True)
+            turned = sb.tile([P, CH], F32, name=f"turned{c}")
+            nc.scalar.copy(out=turned[:], in_=turned_ps[:])
+            rest_ps = psum.tile([P, CH], F32, name=f"rest_ps{c}", tag=("a_ps", "ta_ps0", "ta_ps1")[c])
+            for b in range(CH // P):
+                blk = slice(b * P, (b + 1) * P)
+                nc.tensor.transpose(rest_ps[:, blk], turned[:, blk], ident[:])
+            rest.append(rest_ps)
 
         lead = [sb.tile([P, CH], F32, name=f"lead{c}") for c in range(len(chunks))]
         res = [sb.tile([P, CH], F32, name=f"res{c}") for c in range(len(chunks))]
-        for pair in ((0, 1), (2, 3)):
-            for c in pair:
-                nc.vector.tensor_tensor(lead[c][:], tpa[:, chunks[c]], coef[:, chunks[c]], ALU.mult)
-            for c in pair:
-                if c >= 2:
-                    mid = sb.tile([P, CH], F32, name=f"mid{c}")
-                    nc.vector.tensor_tensor(mid[:], lead[c][:], base_sb[:, chunks[c]], ALU.add)
-                    lead[c] = mid
-            for c in pair:
-                nc.vector.tensor_tensor(res[c][:], lead[c][:], rest[c][:], ALU.add)
-                nc.sync.dma_start(out=out[:, chunks[c]], in_=res[c][:])
+        def finish(c, other):
+            nc.vector.tensor_tensor(res[c][:], other, lead[c][:], ALU.add)
+            nc.sync.dma_start(out=out[:, chunks[c]], in_=res[c][:])
+
+        for c in (0, 1):
+            nc.vector.tensor_tensor(lead[c][:], tpa[:, chunks[c]], coef[:, chunks[c]], ALU.mult)
+        for c in (0, 1):
+            finish(c, rest[c][:])
+        last = sb.tile([P, CH], F32, name="last")
+        nc.vector.tensor_tensor(last[:], terms[3], base_sb[:, chunks[3]], ALU.add)
+        for c in (2, 3):
+            nc.vector.tensor_tensor(lead[c][:], tpa[:, chunks[c]], coef[:, chunks[c]], ALU.mult)
+        finish(2, rest[2][:])
+        finish(3, last[:])

@@ -37,8 +37,11 @@ def tile_attend_ttwopages_kernel(tc, dtab_words, dtab_scales, tab_words, tab_sca
 
         tab_s = sb.tile([P, T], U8, name="tab_s", tag="tab_s", align_bytes=64)
         dtab_s = sb.tile([P, T], U8, name="dtab_s", tag="dtab_s", align_bytes=64)
+        warm_in = reuse.tile([P, 16], F32, name="warm_in", offset=4 * J, align_bytes=64)
+        warm_out = sb.tile([P, 16], F32, name="warm_out", tag="dtab_w", align_bytes=64)
+        nc.vector.memset(warm_in[:], 0.0)
+        nc.scalar.activation(warm_out[:], warm_in[:], ACT.Tanh)
         nc.vector.memset(tab_s[:].bitcast(I32), 0)
-        nc.vector.memset(dtab_s[:].bitcast(I32), 0)
 
         def load_scales(queue, tile, scales):
             for q in range(4):
@@ -46,42 +49,40 @@ def tile_attend_ttwopages_kernel(tc, dtab_words, dtab_scales, tab_words, tab_sca
                                     in_=scales[0, 4 * q:4 * q + 4, :].bitcast(I32))
 
         nc.sync.dma_start(pick[:], offs)
+        nc.sync.dma_start(page_a[:], offs2)
         tab_w = sb.tile([P, T], U16, name="tab_w", tag="tab_w", align_bytes=64)
         nc.sync.dma_start(out=tab_w[:].bitcast(I32), in_=tab_words[0].bitcast(I32))
-        nc.sync.dma_start(page_a[:], offs2)
         nc.sync.dma_start(page_b[:], offs3)
         load_scales(nc.scalar, tab_s, tab_scales)
         w_raw = sb.tile([P, 4, R], F32, name="w_raw")
         nc.sync.dma_start(out=w_raw[:], in_=w1.rearrange("(p t) r -> p t r", t=4))
         dtab_w = sb.tile([P, T], U16, name="dtab_w", tag="dtab_w", align_bytes=64)
         nc.sync.dma_start(out=dtab_w[:].bitcast(I32), in_=dtab_words[0].bitcast(I32))
-        load_scales(nc.sync, dtab_s, dtab_scales)
-        gain_c = sb.tile([P, 1], F32, name="gain_c", tag="a_sb", align_bytes=64)
-        og_c = sb.tile([P, 1], F32, name="og_c")
-        nc.gpsimd.dma_start(out=gain_c[:], in_=gain)
-        nc.gpsimd.dma_start(out=og_c[:], in_=og)
+        gain_c = reuse.tile([P, 1], F32, name="gain_c", offset=4 * J)
+        og_c = reuse.tile([P, 1], F32, name="og_c", offset=4 * J + 32)
+        nc.sync.dma_start(out=gain_c[:], in_=gain)
+        nc.sync.dma_start(out=og_c[:], in_=og)
 
         pb = sb.tile([P, U], F32, name="pb")
-        tpa = sb.tile([P, U], F32, name="tpa")
-        tpb = sb.tile([P, U], F32, name="tpb")
-        for page in (pb, tpb, tpa):
+        pa = sb.tile([P, U], F32, name="pa")
+        for page in (pa, pb):
             nc.vector.memset(page[:], 0.0)
+        nc.vector.memset(dtab_s[:].bitcast(I32), 0)
+        load_scales(nc.sync, dtab_s, dtab_scales)
 
         ident = sb.tile([P, P], F32, name="ident")
         make_identity(nc, ident[:])
-        warm = sb.tile([P, 1], F32, name="warm")
-        nc.scalar.activation(warm[:], pb[:, 0:1], ACT.Tanh)
         w_bf = sb.tile([P, R, 4], BF16, name="w_bf", align_bytes=64)
         nc.scalar.copy(out=w_bf[:], in_=w_raw[:].rearrange("p t r -> p r t"))
         w_codes = sb.tile([P, R], U32, name="w_codes", align_bytes=64)
         w_scales = sb.tile([P, R], U8, name="w_scales", align_bytes=64)
 
-        tab_gw = sb.tile([P, J], U16, name="tab_gw", align_bytes=64)
-        tab_gs = sb.tile([P, J], U8, name="tab_gs", align_bytes=64)
+        tab_gw = sb.tile([P, J], U16, name="tab_gw", tag="tab_gw", align_bytes=64)
+        tab_gs = sb.tile([P, J], U8, name="tab_gs", tag="tab_gs", align_bytes=64)
         nc.vector.tensor_copy(tab_gw[:], tab_w[:].indirect(pick[:]))
+        nc.vector.tensor_copy(tab_gs[:], tab_s[:].indirect(pick[:]))
         nc.vector.quantize_mx(out=w_codes[:].bitcast(FP8X4), scales=w_scales[:],
                               in_=w_bf[:].rearrange("p r t -> p (r t)"))
-        nc.vector.tensor_copy(tab_gs[:], tab_s[:].indirect(pick[:]))
 
         ground_sb = sb.tile([P, U], F32, name="ground_sb", tag="tab_w", align_bytes=64)
         nc.sync.dma_start(out=ground_sb[:], in_=ground)
@@ -99,85 +100,78 @@ def tile_attend_ttwopages_kernel(tc, dtab_words, dtab_scales, tab_words, tab_sca
         nc.scalar.activation(h1[:], a_ps[:], ACT.Copy, scale=gain_c[:])
         nc.scalar.copy(out=a_sb[:], in_=a_ps[:])
 
+        tpb = sb.tile([P, U], F32, name="tpb", tag="tab_gw", align_bytes=64)
+        tpa = sb.tile([P, U], F32, name="tpa", tag="tab_gs", align_bytes=64)
+        for page in (tpb, tpa):
+            nc.gpsimd.memset(page[:], 0.0)
+
         dtab_gw = sb.tile([P, J], U16, name="dtab_gw", align_bytes=64)
         nc.vector.tensor_copy(dtab_gw[:], dtab_w[:].indirect(pick[:]))
-        pa = sb.tile([P, U], F32, name="pa", tag="dtab_w", align_bytes=64)
-        nc.vector.memset(pa[:], 0.0)
         nc.vector.tensor_copy(pa[:].indirect(page_a[:]), h1[:])
         nc.vector.tensor_copy(pb[:].indirect(page_b[:]), a_sb[:])
 
         th = sb.tile([P, U], F32, name="th")
+        arg = sb.tile([P, U], F32, name="arg")
+        sq = sb.tile([P, U], F32, name="sq")
         slope = sb.tile([P, U], F32, name="slope")
-        for h in range(2):
-            cols = slice(h * J, (h + 1) * J)
-            arg = sb.tile([P, J], F32, name=f"arg{h}", tag=f"arg{h}")
-            sq = sb.tile([P, J], F32, name=f"sq{h}", tag=f"sq{h}")
-            nc.gpsimd.tensor_tensor(arg[:], pa[:, cols], ground_sb[:, cols], ALU.add)
-            nc.scalar.activation(th[:, cols], arg[:], ACT.Tanh)
-            nc.scalar.activation(sq[:], th[:, cols], ACT.Square)
-            nc.scalar.activation(slope[:, cols], sq[:], ACT.Copy, scale=-1.0, bias=1.0)
+        left, right = slice(0, J), slice(J, U)
+        for cols in (left, right):
+            nc.gpsimd.tensor_tensor(arg[:, cols], pa[:, cols], ground_sb[:, cols], ALU.add)
+        nc.scalar.activation(th[:, left], arg[:, left], ACT.Tanh)
+        nc.scalar.activation(sq[:, left], th[:, left], ACT.Square)
+        nc.scalar.activation(th[:, right], arg[:, right], ACT.Tanh)
+        nc.scalar.activation(slope[:, left], sq[:, left], ACT.Copy, scale=-1.0, bias=1.0)
+        nc.scalar.activation(sq[:, right], th[:, right], ACT.Square)
 
-        ta_og = []
         ta_ps = []
         for h in range(2):
-            slots = slice(h * HALF, (h + 1) * HALF)
             gs = reuse.tile([P, HALF], U8, name=f"dtab_gs{h}", offset=h * HALF, align_bytes=64)
             nc.vector.tensor_copy(gs[:], dtab_s[:].indirect(pick[:, h * HALF // 16:(h + 1) * HALF // 16]))
-            ta_ps.append(psum.tile([P, HALF], F32, name=f"ta_ps{h}", tag=f"ta_ps{h}"))
+            ta_ps.append(psum.tile([P, HALF], F32, name=f"ta_ps{h}"))
             nc.tensor.matmul_mx(out=ta_ps[h][:], lhsT=w_codes[:].bitcast(FP8X4), lhsT_scale=w_scales[:],
-                                rhs=dtab_gw[:, slots].bitcast(FP4X4), rhs_scale=gs[:], start=True, stop=True)
-            ta_og.append(arg[:, slots])
-            nc.scalar.activation(ta_og[h], ta_ps[h][:], ACT.Copy, scale=og_c[:])
-        th1_og = sq
+                                rhs=dtab_gw[:, h * HALF:(h + 1) * HALF].bitcast(FP4X4), rhs_scale=gs[:],
+                                start=True, stop=True)
+        ta_og = [arg[:, J + h * HALF:J + (h + 1) * HALF] for h in range(2)]
+        nc.scalar.activation(ta_og[0], ta_ps[0][:], ACT.Copy, scale=og_c[:])
+        nc.scalar.activation(slope[:, right], sq[:, right], ACT.Copy, scale=-1.0, bias=1.0)
+        nc.scalar.activation(ta_og[1], ta_ps[1][:], ACT.Copy, scale=og_c[:])
+        th1_og = sq[:, right]
         for h in range(2):
             nc.scalar.activation(th1_og[:, h * HALF:(h + 1) * HALF], ta_ps[h][:], ACT.Copy, scale=gain_og[:])
 
         coef = sb.tile([P, U], F32, name="coef")
-        for h in range(2):
-            cols = slice(h * J, (h + 1) * J)
-            second = sb.tile([P, J], F32, name=f"second{h}", tag=f"second{h}")
-            nc.gpsimd.tensor_tensor(second[:], pb[:, cols], ground_sb[:, cols], ALU.add)
-            nc.gpsimd.tensor_tensor(coef[:, cols], second[:], slope[:, cols], ALU.mult)
+        second = sb.tile([P, U], F32, name="second")
+        nc.gpsimd.tensor_tensor(second[:], pb[:], ground_sb[:], ALU.add)
+        nc.gpsimd.tensor_tensor(coef[:], second[:], slope[:], ALU.mult)
 
         for h in range(2):
             nc.vector.tensor_copy(tpb[:].indirect(page_b[:, h * HALF // 16:(h + 1) * HALF // 16]), ta_og[h])
-        nc.vector.tensor_copy(tpa[:].indirect(page_a[:]), th1_og[:])
+        nc.vector.tensor_copy(tpa[:].indirect(page_a[:]), th1_og)
 
-        chunks = [slice(c * CH, (c + 1) * CH) for c in range(U // CH)]
-        terms = [second[:, :CH], second[:, CH:], slope[:, J:J + CH], slope[:, J + CH:]]
+        term = second
+        pieces = [slice(0, 384), slice(384, 768), slice(768, U)]
+        turned_ps = []
+        for c, cols in enumerate(pieces):
+            turned_ps.append(psum.tile([P, cols.stop - cols.start], F32, name=f"turned_ps{c}"))
+            for b in range(cols.start, cols.stop, P):
+                nc.tensor.matmul(turned_ps[c][:, b - cols.start:b - cols.start + P], base_sb[:, b:b + P], ident[:],
+                                 start=(b == cols.start), stop=False, is_transpose=True)
         rest = []
-        for c, cols in enumerate(chunks):
-            nc.gpsimd.tensor_tensor(terms[c], tpb[:, cols], th[:, cols], ALU.mult)
-            if c == 3:
-                break
-            turned_ps = psum.tile([P, CH], F32, name=f"turned_ps{c}", tag="turned_ps", bufs=2)
-            for b in range(CH // P):
-                blk = slice(b * P, (b + 1) * P)
-                nc.tensor.matmul(turned_ps[:, blk], base_sb[:, c * CH + b * P:c * CH + (b + 1) * P], ident[:],
-                                 start=True, stop=False, is_transpose=True)
-                nc.tensor.matmul(turned_ps[:, blk], terms[c][:, blk], ident[:],
-                                 start=False, stop=True, is_transpose=True)
-            turned = sb.tile([P, CH], F32, name=f"turned{c}")
-            nc.scalar.copy(out=turned[:], in_=turned_ps[:])
-            rest_ps = psum.tile([P, CH], F32, name=f"rest_ps{c}", tag=("a_ps", "ta_ps0", "ta_ps1")[c])
-            for b in range(CH // P):
-                blk = slice(b * P, (b + 1) * P)
-                nc.tensor.transpose(rest_ps[:, blk], turned[:, blk], ident[:])
-            rest.append(rest_ps)
+        for c, cols in enumerate(pieces):
+            width = cols.stop - cols.start
+            nc.gpsimd.tensor_tensor(term[:, cols], tpb[:, cols], th[:, cols], ALU.mult)
+            for b in range(cols.start, cols.stop, P):
+                nc.tensor.matmul(turned_ps[c][:, b - cols.start:b - cols.start + P], term[:, b:b + P], ident[:],
+                                 start=False, stop=(b == cols.stop - P), is_transpose=True)
+            turned = sb.tile([P, width], F32, name=f"turned{c}")
+            nc.scalar.copy(out=turned[:], in_=turned_ps[c][:])
+            rest.append(psum.tile([P, width], F32, name=f"rest_ps{c}", tag=("a_ps", "rest1", "rest2")[c]))
+            for b in range(0, width, P):
+                nc.tensor.transpose(rest[c][:, b:b + P], turned[:, b:b + P], ident[:])
 
-        lead = [sb.tile([P, CH], F32, name=f"lead{c}") for c in range(len(chunks))]
-        res = [sb.tile([P, CH], F32, name=f"res{c}") for c in range(len(chunks))]
-        def finish(c, other):
-            nc.vector.tensor_tensor(res[c][:], other, lead[c][:], ALU.add)
-            nc.sync.dma_start(out=out[:, chunks[c]], in_=res[c][:])
-
-        for c in (0, 1):
-            nc.vector.tensor_tensor(lead[c][:], tpa[:, chunks[c]], coef[:, chunks[c]], ALU.mult)
-        for c in (0, 1):
-            finish(c, rest[c][:])
-        last = sb.tile([P, CH], F32, name="last")
-        nc.vector.tensor_tensor(last[:], terms[3], base_sb[:, chunks[3]], ALU.add)
-        for c in (2, 3):
-            nc.vector.tensor_tensor(lead[c][:], tpa[:, chunks[c]], coef[:, chunks[c]], ALU.mult)
-        finish(2, rest[2][:])
-        finish(3, last[:])
+        lead = sb.tile([P, U], F32, name="lead")
+        nc.vector.tensor_tensor(lead[:], tpa[:], coef[:], ALU.mult)
+        for c, cols in enumerate(pieces):
+            res = sb.tile([P, cols.stop - cols.start], F32, name=f"res{c}")
+            nc.vector.tensor_tensor(res[:], rest[c][:], lead[:, cols], ALU.add)
+            nc.sync.dma_start(out=out[:, cols], in_=res[:])

@@ -18,8 +18,25 @@ ACT = mybir.ActivationFunctionType
 ALU = mybir.AluOpType
 
 P = 128
+PACK = 4
+STRIPE = 16
+QUADRANTS, SCALE_ROWS = 4, 4
 HALF = J // 2
-CH = 256
+SLOT_HALVES = (slice(0, HALF), slice(HALF, J))
+LEFT, RIGHT = slice(0, U // 2), slice(U // 2, U)
+PIECES = (slice(0, 384), slice(384, 768), slice(768, U))
+H1_BYTES = 4 * J
+BLOCK_BYTES = 32
+
+
+def entries(list_tile, slots):
+    return list_tile[:, slots.start // STRIPE:slots.stop // STRIPE]
+
+
+def load_scale_rows(queue, tile, scales):
+    for quad in range(QUADRANTS):
+        queue.dma_start(out=tile[32 * quad:32 * quad + SCALE_ROWS, :].bitcast(I32),
+                        in_=scales[0, SCALE_ROWS * quad:SCALE_ROWS * (quad + 1), :].bitcast(I32))
 
 
 def tile_attend_ttwopages_kernel(tc, dtab_words, dtab_scales, tab_words, tab_scales, w1, gain, ground, og, base,
@@ -28,61 +45,62 @@ def tile_attend_ttwopages_kernel(tc, dtab_words, dtab_scales, tab_words, tab_sca
     with ExitStack() as ctx:
         lists = ctx.enter_context(tc.tile_pool(name="lists", bufs=1))
         sb = ctx.enter_context(tc.tile_pool(name="sb", bufs=1))
-        reuse = ctx.enter_context(tc.tile_pool(name="reuse", bufs=1))
+        placed = ctx.enter_context(tc.tile_pool(name="placed", bufs=1))
         psum = ctx.enter_context(tc.psum_pool(name="psum", bufs=1))
 
-        pick = lists.tile([P, J // 16], U16, name="pick")
-        page_a = lists.tile([P, J // 16], U16, name="page_a")
-        page_b = lists.tile([P, J // 16], U16, name="page_b")
+        idx = lists.tile([P, J // STRIPE], U16, name="idx")
+        idx2 = lists.tile([P, J // STRIPE], U16, name="idx2")
+        idx3 = lists.tile([P, J // STRIPE], U16, name="idx3")
 
         tab_s = sb.tile([P, T], U8, name="tab_s", tag="tab_s", align_bytes=64)
-        dtab_s = sb.tile([P, T], U8, name="dtab_s", tag="dtab_s", align_bytes=64)
-        warm_in = reuse.tile([P, 16], F32, name="warm_in", offset=4 * J, align_bytes=64)
-        warm_out = sb.tile([P, 16], F32, name="warm_out", tag="dtab_w", align_bytes=64)
+        dtab_s = sb.tile([P, T], U8, name="dtab_s", align_bytes=64)
+
+        warm_in = placed.tile([P, 2 * BLOCK_BYTES // 4], F32, name="warm_in", offset=H1_BYTES, align_bytes=64)
+        warm_out = sb.tile([P, 2 * BLOCK_BYTES // 4], F32, name="warm_out", tag="dtab_w", align_bytes=64)
         nc.vector.memset(warm_in[:], 0.0)
         nc.scalar.activation(warm_out[:], warm_in[:], ACT.Tanh)
+
         nc.vector.memset(tab_s[:].bitcast(I32), 0)
-
-        def load_scales(queue, tile, scales):
-            for q in range(4):
-                queue.dma_start(out=tile[32 * q:32 * q + 4, :].bitcast(I32),
-                                    in_=scales[0, 4 * q:4 * q + 4, :].bitcast(I32))
-
-        nc.sync.dma_start(pick[:], offs)
-        nc.sync.dma_start(page_a[:], offs2)
+        nc.sync.dma_start(idx[:], offs)
+        nc.sync.dma_start(idx2[:], offs2)
         tab_w = sb.tile([P, T], U16, name="tab_w", tag="tab_w", align_bytes=64)
         nc.sync.dma_start(out=tab_w[:].bitcast(I32), in_=tab_words[0].bitcast(I32))
-        nc.sync.dma_start(page_b[:], offs3)
-        load_scales(nc.scalar, tab_s, tab_scales)
-        w_raw = sb.tile([P, 4, R], F32, name="w_raw")
-        nc.sync.dma_start(out=w_raw[:], in_=w1.rearrange("(p t) r -> p t r", t=4))
+        nc.sync.dma_start(idx3[:], offs3)
+        load_scale_rows(nc.scalar, tab_s, tab_scales)
+        w_raw = sb.tile([P, PACK, R], F32, name="w_raw")
+        nc.sync.dma_start(out=w_raw[:], in_=w1.rearrange("(p t) r -> p t r", t=PACK))
         dtab_w = sb.tile([P, T], U16, name="dtab_w", tag="dtab_w", align_bytes=64)
         nc.sync.dma_start(out=dtab_w[:].bitcast(I32), in_=dtab_words[0].bitcast(I32))
-        gain_c = reuse.tile([P, 1], F32, name="gain_c", offset=4 * J)
-        og_c = reuse.tile([P, 1], F32, name="og_c", offset=4 * J + 32)
-        nc.sync.dma_start(out=gain_c[:], in_=gain)
-        nc.sync.dma_start(out=og_c[:], in_=og)
+        gain_col = placed.tile([P, 1], F32, name="gain_col", offset=H1_BYTES)
+        og_col = placed.tile([P, 1], F32, name="og_col", offset=H1_BYTES + BLOCK_BYTES)
+        nc.sync.dma_start(out=gain_col[:], in_=gain)
+        nc.sync.dma_start(out=og_col[:], in_=og)
 
         pb = sb.tile([P, U], F32, name="pb")
         pa = sb.tile([P, U], F32, name="pa")
         for page in (pa, pb):
             nc.vector.memset(page[:], 0.0)
         nc.vector.memset(dtab_s[:].bitcast(I32), 0)
-        load_scales(nc.sync, dtab_s, dtab_scales)
+        load_scale_rows(nc.sync, dtab_s, dtab_scales)
 
         ident = sb.tile([P, P], F32, name="ident")
         make_identity(nc, ident[:])
-        w_bf = sb.tile([P, R, 4], BF16, name="w_bf", align_bytes=64)
+
+        w_bf = sb.tile([P, R, PACK], BF16, name="w_bf", align_bytes=64)
         nc.scalar.copy(out=w_bf[:], in_=w_raw[:].rearrange("p t r -> p r t"))
         w_codes = sb.tile([P, R], U32, name="w_codes", align_bytes=64)
         w_scales = sb.tile([P, R], U8, name="w_scales", align_bytes=64)
 
         tab_gw = sb.tile([P, J], U16, name="tab_gw", tag="tab_gw", align_bytes=64)
         tab_gs = sb.tile([P, J], U8, name="tab_gs", tag="tab_gs", align_bytes=64)
-        nc.vector.tensor_copy(tab_gw[:], tab_w[:].indirect(pick[:]))
-        nc.vector.tensor_copy(tab_gs[:], tab_s[:].indirect(pick[:]))
+        nc.vector.tensor_copy(tab_gw[:], tab_w[:].indirect(idx[:]))
+        nc.vector.tensor_copy(tab_gs[:], tab_s[:].indirect(idx[:]))
         nc.vector.quantize_mx(out=w_codes[:].bitcast(FP8X4), scales=w_scales[:],
                               in_=w_bf[:].rearrange("p r t -> p (r t)"))
+
+        def product(acc, words, scales):
+            nc.tensor.matmul_mx(out=acc, lhsT=w_codes[:].bitcast(FP8X4), lhsT_scale=w_scales[:],
+                                rhs=words.bitcast(FP4X4), rhs_scale=scales, start=True, stop=True)
 
         ground_sb = sb.tile([P, U], F32, name="ground_sb", tag="tab_w", align_bytes=64)
         nc.sync.dma_start(out=ground_sb[:], in_=ground)
@@ -90,15 +108,17 @@ def tile_attend_ttwopages_kernel(tc, dtab_words, dtab_scales, tab_words, tab_sca
         nc.sync.dma_start(out=base_sb[:], in_=base)
 
         gain_og = sb.tile([P, 1], F32, name="gain_og")
-        nc.scalar.activation(gain_og[:], gain_c[:], ACT.Copy, scale=og_c[:])
+        nc.scalar.activation(gain_og[:], gain_col[:], ACT.Copy, scale=og_col[:])
 
-        a_ps = psum.tile([P, J], F32, name="a_ps", tag="a_ps")
-        nc.tensor.matmul_mx(out=a_ps[:], lhsT=w_codes[:].bitcast(FP8X4), lhsT_scale=w_scales[:],
-                            rhs=tab_gw[:].bitcast(FP4X4), rhs_scale=tab_gs[:], start=True, stop=True)
-        h1 = reuse.tile([P, J], F32, name="h1", offset=0, align_bytes=64)
-        a_sb = sb.tile([P, J], F32, name="a_sb", tag="a_sb", align_bytes=64)
-        nc.scalar.activation(h1[:], a_ps[:], ACT.Copy, scale=gain_c[:])
-        nc.scalar.copy(out=a_sb[:], in_=a_ps[:])
+        h1 = placed.tile([P, J], F32, name="h1", offset=0, align_bytes=64)
+        a_sb = sb.tile([P, J], F32, name="a_sb")
+        a_ps = []
+        for h, slots in enumerate(SLOT_HALVES):
+            a_ps.append(psum.tile([P, HALF], F32, name=f"a_ps{h}", tag=f"a_ps{h}"))
+            product(a_ps[h][:], tab_gw[:, slots], tab_gs[:, slots])
+            nc.scalar.activation(h1[:, slots], a_ps[h][:], ACT.Copy, scale=gain_col[:])
+        for h, slots in enumerate(SLOT_HALVES):
+            nc.scalar.copy(out=a_sb[:, slots], in_=a_ps[h][:])
 
         tpb = sb.tile([P, U], F32, name="tpb", tag="tab_gw", align_bytes=64)
         tpa = sb.tile([P, U], F32, name="tpa", tag="tab_gs", align_bytes=64)
@@ -106,72 +126,71 @@ def tile_attend_ttwopages_kernel(tc, dtab_words, dtab_scales, tab_words, tab_sca
             nc.gpsimd.memset(page[:], 0.0)
 
         dtab_gw = sb.tile([P, J], U16, name="dtab_gw", align_bytes=64)
-        nc.vector.tensor_copy(dtab_gw[:], dtab_w[:].indirect(pick[:]))
-        nc.vector.tensor_copy(pa[:].indirect(page_a[:]), h1[:])
-        nc.vector.tensor_copy(pb[:].indirect(page_b[:]), a_sb[:])
+        nc.vector.tensor_copy(dtab_gw[:], dtab_w[:].indirect(idx[:]))
+        for slots in SLOT_HALVES:
+            nc.vector.tensor_copy(pa[:].indirect(entries(idx2, slots)), h1[:, slots])
+        nc.vector.tensor_copy(pb[:].indirect(idx3[:]), a_sb[:])
 
         th = sb.tile([P, U], F32, name="th")
         arg = sb.tile([P, U], F32, name="arg")
         sq = sb.tile([P, U], F32, name="sq")
         slope = sb.tile([P, U], F32, name="slope")
-        left, right = slice(0, J), slice(J, U)
-        for cols in (left, right):
+        for cols in (LEFT, RIGHT):
             nc.gpsimd.tensor_tensor(arg[:, cols], pa[:, cols], ground_sb[:, cols], ALU.add)
-        nc.scalar.activation(th[:, left], arg[:, left], ACT.Tanh)
-        nc.scalar.activation(sq[:, left], th[:, left], ACT.Square)
-        nc.scalar.activation(th[:, right], arg[:, right], ACT.Tanh)
-        nc.scalar.activation(slope[:, left], sq[:, left], ACT.Copy, scale=-1.0, bias=1.0)
-        nc.scalar.activation(sq[:, right], th[:, right], ACT.Square)
+        nc.scalar.activation(th[:, LEFT], arg[:, LEFT], ACT.Tanh)
+        nc.scalar.activation(sq[:, LEFT], th[:, LEFT], ACT.Square)
+        nc.scalar.activation(th[:, RIGHT], arg[:, RIGHT], ACT.Tanh)
+        nc.scalar.activation(slope[:, LEFT], sq[:, LEFT], ACT.Copy, scale=-1.0, bias=1.0)
+        nc.scalar.activation(sq[:, RIGHT], th[:, RIGHT], ACT.Square)
 
         ta_ps = []
-        for h in range(2):
-            gs = reuse.tile([P, HALF], U8, name=f"dtab_gs{h}", offset=h * HALF, align_bytes=64)
-            nc.vector.tensor_copy(gs[:], dtab_s[:].indirect(pick[:, h * HALF // 16:(h + 1) * HALF // 16]))
+        for h, slots in enumerate(SLOT_HALVES):
+            dtab_gs = placed.tile([P, HALF], U8, name=f"dtab_gs{h}", offset=slots.start, align_bytes=64)
+            nc.vector.tensor_copy(dtab_gs[:], dtab_s[:].indirect(entries(idx, slots)))
             ta_ps.append(psum.tile([P, HALF], F32, name=f"ta_ps{h}"))
-            nc.tensor.matmul_mx(out=ta_ps[h][:], lhsT=w_codes[:].bitcast(FP8X4), lhsT_scale=w_scales[:],
-                                rhs=dtab_gw[:, h * HALF:(h + 1) * HALF].bitcast(FP4X4), rhs_scale=gs[:],
-                                start=True, stop=True)
-        ta_og = [arg[:, J + h * HALF:J + (h + 1) * HALF] for h in range(2)]
-        nc.scalar.activation(ta_og[0], ta_ps[0][:], ACT.Copy, scale=og_c[:])
-        nc.scalar.activation(slope[:, right], sq[:, right], ACT.Copy, scale=-1.0, bias=1.0)
-        nc.scalar.activation(ta_og[1], ta_ps[1][:], ACT.Copy, scale=og_c[:])
-        th1_og = sq[:, right]
-        for h in range(2):
-            nc.scalar.activation(th1_og[:, h * HALF:(h + 1) * HALF], ta_ps[h][:], ACT.Copy, scale=gain_og[:])
+            product(ta_ps[h][:], dtab_gw[:, slots], dtab_gs[:])
+
+        ta_og = arg[:, RIGHT]
+        th1_og = sq[:, RIGHT]
+        nc.scalar.activation(ta_og[:, SLOT_HALVES[0]], ta_ps[0][:], ACT.Copy, scale=og_col[:])
+        nc.scalar.activation(slope[:, RIGHT], sq[:, RIGHT], ACT.Copy, scale=-1.0, bias=1.0)
+        nc.scalar.activation(ta_og[:, SLOT_HALVES[1]], ta_ps[1][:], ACT.Copy, scale=og_col[:])
+        for h, slots in enumerate(SLOT_HALVES):
+            nc.scalar.activation(th1_og[:, slots], ta_ps[h][:], ACT.Copy, scale=gain_og[:])
 
         coef = sb.tile([P, U], F32, name="coef")
-        second = sb.tile([P, U], F32, name="second")
-        nc.gpsimd.tensor_tensor(second[:], pb[:], ground_sb[:], ALU.add)
-        nc.gpsimd.tensor_tensor(coef[:], second[:], slope[:], ALU.mult)
+        pb_ground = sb.tile([P, U], F32, name="pb_ground")
+        nc.gpsimd.tensor_tensor(pb_ground[:], pb[:], ground_sb[:], ALU.add)
+        nc.gpsimd.tensor_tensor(coef[:], pb_ground[:], slope[:], ALU.mult)
 
-        for h in range(2):
-            nc.vector.tensor_copy(tpb[:].indirect(page_b[:, h * HALF // 16:(h + 1) * HALF // 16]), ta_og[h])
-        nc.vector.tensor_copy(tpa[:].indirect(page_a[:]), th1_og)
+        for slots in SLOT_HALVES:
+            nc.vector.tensor_copy(tpb[:].indirect(entries(idx3, slots)), ta_og[:, slots])
+        nc.vector.tensor_copy(tpa[:].indirect(idx2[:]), th1_og)
 
-        term = second
-        pieces = [slice(0, 384), slice(384, 768), slice(768, U)]
         turned_ps = []
-        for c, cols in enumerate(pieces):
+        for c, cols in enumerate(PIECES):
             turned_ps.append(psum.tile([P, cols.stop - cols.start], F32, name=f"turned_ps{c}"))
             for b in range(cols.start, cols.stop, P):
                 nc.tensor.matmul(turned_ps[c][:, b - cols.start:b - cols.start + P], base_sb[:, b:b + P], ident[:],
                                  start=(b == cols.start), stop=False, is_transpose=True)
-        rest = []
-        for c, cols in enumerate(pieces):
+        tpb_th = pb_ground
+        rest_banks = ("a_ps0", "a_ps1", "rest_ps2")
+        rest_ps = []
+        for c, cols in enumerate(PIECES):
             width = cols.stop - cols.start
-            nc.gpsimd.tensor_tensor(term[:, cols], tpb[:, cols], th[:, cols], ALU.mult)
+            nc.gpsimd.tensor_tensor(tpb_th[:, cols], tpb[:, cols], th[:, cols], ALU.mult)
             for b in range(cols.start, cols.stop, P):
-                nc.tensor.matmul(turned_ps[c][:, b - cols.start:b - cols.start + P], term[:, b:b + P], ident[:],
+                nc.tensor.matmul(turned_ps[c][:, b - cols.start:b - cols.start + P], tpb_th[:, b:b + P], ident[:],
                                  start=False, stop=(b == cols.stop - P), is_transpose=True)
             turned = sb.tile([P, width], F32, name=f"turned{c}")
             nc.scalar.copy(out=turned[:], in_=turned_ps[c][:])
-            rest.append(psum.tile([P, width], F32, name=f"rest_ps{c}", tag=("a_ps", "rest1", "rest2")[c]))
+            rest_ps.append(psum.tile([P, width], F32, name=f"rest_ps{c}", tag=rest_banks[c]))
             for b in range(0, width, P):
-                nc.tensor.transpose(rest[c][:, b:b + P], turned[:, b:b + P], ident[:])
+                nc.tensor.transpose(rest_ps[c][:, b:b + P], turned[:, b:b + P], ident[:])
 
         lead = sb.tile([P, U], F32, name="lead")
         nc.vector.tensor_tensor(lead[:], tpa[:], coef[:], ALU.mult)
-        for c, cols in enumerate(pieces):
+        for c, cols in enumerate(PIECES):
             res = sb.tile([P, cols.stop - cols.start], F32, name=f"res{c}")
-            nc.vector.tensor_tensor(res[:], rest[c][:], lead[:, cols], ALU.add)
+            nc.vector.tensor_tensor(res[:], rest_ps[c][:], lead[:, cols], ALU.add)
             nc.sync.dma_start(out=out[:, cols], in_=res[:])

from contextlib import ExitStack

import concourse.mybir as mybir
from concourse.masks import make_identity

K, R, T, J, U = 512, 128, 2048, 512, 1024
FLOPS = 2 * 2 * K * R * J

F32 = mybir.dt.float32
BF16 = mybir.dt.bfloat16
I32 = mybir.dt.int32
U32 = mybir.dt.uint32
U16 = mybir.dt.uint16
U8 = mybir.dt.uint8
FP8X4 = mybir.dt.float8_e4m3fn_x4
FP4X4 = mybir.dt.float4_e2m1fn_x4
ACT = mybir.ActivationFunctionType
ALU = mybir.AluOpType

P = 128
PACK = 4
STRIPE = 16
QUADRANTS, SCALE_ROWS = 4, 4
HALF = J // 2
SLOT_HALVES = (slice(0, HALF), slice(HALF, J))
LEFT, RIGHT = slice(0, U // 2), slice(U // 2, U)
PIECES = (slice(0, 384), slice(384, 768), slice(768, U))
H1_BYTES = 4 * J
BLOCK_BYTES = 32


def entries(list_tile, slots):
    return list_tile[:, slots.start // STRIPE:slots.stop // STRIPE]


def load_scale_rows(queue, tile, scales):
    for quad in range(QUADRANTS):
        queue.dma_start(out=tile[32 * quad:32 * quad + SCALE_ROWS, :].bitcast(I32),
                        in_=scales[0, SCALE_ROWS * quad:SCALE_ROWS * (quad + 1), :].bitcast(I32))


def tile_attend_ttwopages_kernel(tc, dtab_words, dtab_scales, tab_words, tab_scales, w1, gain, ground, og, base,
                                  offs, offs2, offs3, out):
    nc = tc.nc
    with ExitStack() as ctx:
        lists = ctx.enter_context(tc.tile_pool(name="lists", bufs=1))
        sb = ctx.enter_context(tc.tile_pool(name="sb", bufs=1))
        placed = ctx.enter_context(tc.tile_pool(name="placed", bufs=1))
        psum = ctx.enter_context(tc.psum_pool(name="psum", bufs=1))

        idx = lists.tile([P, J // STRIPE], U16, name="idx")
        idx2 = lists.tile([P, J // STRIPE], U16, name="idx2")
        idx3 = lists.tile([P, J // STRIPE], U16, name="idx3")

        tab_s = sb.tile([P, T], U8, name="tab_s", tag="tab_s", align_bytes=64)
        dtab_s = sb.tile([P, T], U8, name="dtab_s", align_bytes=64)

        warm_in = placed.tile([P, 2 * BLOCK_BYTES // 4], F32, name="warm_in", offset=H1_BYTES, align_bytes=64)
        warm_out = sb.tile([P, 2 * BLOCK_BYTES // 4], F32, name="warm_out", tag="dtab_w", align_bytes=64)
        nc.vector.memset(warm_in[:], 0.0)
        nc.scalar.activation(warm_out[:], warm_in[:], ACT.Tanh)

        nc.vector.memset(tab_s[:].bitcast(I32), 0)
        nc.sync.dma_start(idx[:], offs)
        nc.sync.dma_start(idx2[:], offs2)
        tab_w = sb.tile([P, T], U16, name="tab_w", tag="tab_w", align_bytes=64)
        nc.sync.dma_start(out=tab_w[:].bitcast(I32), in_=tab_words[0].bitcast(I32))
        nc.sync.dma_start(idx3[:], offs3)
        load_scale_rows(nc.scalar, tab_s, tab_scales)
        w_raw = sb.tile([P, PACK, R], F32, name="w_raw")
        nc.sync.dma_start(out=w_raw[:], in_=w1.rearrange("(p t) r -> p t r", t=PACK))
        dtab_w = sb.tile([P, T], U16, name="dtab_w", tag="dtab_w", align_bytes=64)
        nc.sync.dma_start(out=dtab_w[:].bitcast(I32), in_=dtab_words[0].bitcast(I32))
        gain_col = placed.tile([P, 1], F32, name="gain_col", offset=H1_BYTES)
        og_col = placed.tile([P, 1], F32, name="og_col", offset=H1_BYTES + BLOCK_BYTES)
        nc.sync.dma_start(out=gain_col[:], in_=gain)
        nc.sync.dma_start(out=og_col[:], in_=og)

        pb = sb.tile([P, U], F32, name="pb")
        pa = sb.tile([P, U], F32, name="pa")
        for page in (pa, pb):
            nc.vector.memset(page[:], 0.0)
        nc.vector.memset(dtab_s[:].bitcast(I32), 0)
        load_scale_rows(nc.sync, dtab_s, dtab_scales)

        ident = sb.tile([P, P], F32, name="ident")
        make_identity(nc, ident[:])

        w_bf = sb.tile([P, R, PACK], BF16, name="w_bf", align_bytes=64)
        nc.scalar.copy(out=w_bf[:], in_=w_raw[:].rearrange("p t r -> p r t"))
        w_codes = sb.tile([P, R], U32, name="w_codes", align_bytes=64)
        w_scales = sb.tile([P, R], U8, name="w_scales", align_bytes=64)

        tab_gw = sb.tile([P, J], U16, name="tab_gw", tag="tab_gw", align_bytes=64)
        tab_gs = sb.tile([P, J], U8, name="tab_gs", tag="tab_gs", align_bytes=64)
        nc.vector.tensor_copy(tab_gw[:], tab_w[:].indirect(idx[:]))
        nc.vector.tensor_copy(tab_gs[:], tab_s[:].indirect(idx[:]))
        nc.vector.quantize_mx(out=w_codes[:].bitcast(FP8X4), scales=w_scales[:],
                              in_=w_bf[:].rearrange("p r t -> p (r t)"))

        def product(acc, words, scales):
            nc.tensor.matmul_mx(out=acc, lhsT=w_codes[:].bitcast(FP8X4), lhsT_scale=w_scales[:],
                                rhs=words.bitcast(FP4X4), rhs_scale=scales, start=True, stop=True)

        ground_sb = sb.tile([P, U], F32, name="ground_sb", tag="tab_w", align_bytes=64)
        nc.sync.dma_start(out=ground_sb[:], in_=ground)
        base_sb = sb.tile([P, U], F32, name="base_sb", tag="tab_s", align_bytes=64)
        nc.sync.dma_start(out=base_sb[:], in_=base)

        gain_og = sb.tile([P, 1], F32, name="gain_og")
        nc.scalar.activation(gain_og[:], gain_col[:], ACT.Copy, scale=og_col[:])

        h1 = placed.tile([P, J], F32, name="h1", offset=0, align_bytes=64)
        a_sb = sb.tile([P, J], F32, name="a_sb")
        a_ps = []
        for h, slots in enumerate(SLOT_HALVES):
            a_ps.append(psum.tile([P, HALF], F32, name=f"a_ps{h}", tag=f"a_ps{h}"))
            product(a_ps[h][:], tab_gw[:, slots], tab_gs[:, slots])
            nc.scalar.activation(h1[:, slots], a_ps[h][:], ACT.Copy, scale=gain_col[:])
        for h, slots in enumerate(SLOT_HALVES):
            nc.scalar.copy(out=a_sb[:, slots], in_=a_ps[h][:])

        tpb = sb.tile([P, U], F32, name="tpb", tag="tab_gw", align_bytes=64)
        tpa = sb.tile([P, U], F32, name="tpa", tag="tab_gs", align_bytes=64)
        for page in (tpb, tpa):
            nc.gpsimd.memset(page[:], 0.0)

        dtab_gw = sb.tile([P, J], U16, name="dtab_gw", align_bytes=64)
        nc.vector.tensor_copy(dtab_gw[:], dtab_w[:].indirect(idx[:]))
        for slots in SLOT_HALVES:
            nc.vector.tensor_copy(pa[:].indirect(entries(idx2, slots)), h1[:, slots])
        nc.vector.tensor_copy(pb[:].indirect(idx3[:]), a_sb[:])

        th = sb.tile([P, U], F32, name="th")
        arg = sb.tile([P, U], F32, name="arg")
        sq = sb.tile([P, U], F32, name="sq")
        slope = sb.tile([P, U], F32, name="slope")
        for cols in (LEFT, RIGHT):
            nc.gpsimd.tensor_tensor(arg[:, cols], pa[:, cols], ground_sb[:, cols], ALU.add)
        nc.scalar.activation(th[:, LEFT], arg[:, LEFT], ACT.Tanh)
        nc.scalar.activation(sq[:, LEFT], th[:, LEFT], ACT.Square)
        nc.scalar.activation(th[:, RIGHT], arg[:, RIGHT], ACT.Tanh)
        nc.scalar.activation(slope[:, LEFT], sq[:, LEFT], ACT.Copy, scale=-1.0, bias=1.0)
        nc.scalar.activation(sq[:, RIGHT], th[:, RIGHT], ACT.Square)

        ta_ps = []
        for h, slots in enumerate(SLOT_HALVES):
            dtab_gs = placed.tile([P, HALF], U8, name=f"dtab_gs{h}", offset=slots.start, align_bytes=64)
            nc.vector.tensor_copy(dtab_gs[:], dtab_s[:].indirect(entries(idx, slots)))
            ta_ps.append(psum.tile([P, HALF], F32, name=f"ta_ps{h}"))
            product(ta_ps[h][:], dtab_gw[:, slots], dtab_gs[:])

        ta_og = arg[:, RIGHT]
        th1_og = sq[:, RIGHT]
        nc.scalar.activation(ta_og[:, SLOT_HALVES[0]], ta_ps[0][:], ACT.Copy, scale=og_col[:])
        nc.scalar.activation(slope[:, RIGHT], sq[:, RIGHT], ACT.Copy, scale=-1.0, bias=1.0)
        nc.scalar.activation(ta_og[:, SLOT_HALVES[1]], ta_ps[1][:], ACT.Copy, scale=og_col[:])
        for h, slots in enumerate(SLOT_HALVES):
            nc.scalar.activation(th1_og[:, slots], ta_ps[h][:], ACT.Copy, scale=gain_og[:])

        coef = sb.tile([P, U], F32, name="coef")
        pb_ground = sb.tile([P, U], F32, name="pb_ground")
        nc.gpsimd.tensor_tensor(pb_ground[:], pb[:], ground_sb[:], ALU.add)
        nc.gpsimd.tensor_tensor(coef[:], pb_ground[:], slope[:], ALU.mult)

        for slots in SLOT_HALVES:
            nc.vector.tensor_copy(tpb[:].indirect(entries(idx3, slots)), ta_og[:, slots])
        nc.vector.tensor_copy(tpa[:].indirect(idx2[:]), th1_og)

        turned_ps = []
        for c, cols in enumerate(PIECES):
            turned_ps.append(psum.tile([P, cols.stop - cols.start], F32, name=f"turned_ps{c}"))
            for b in range(cols.start, cols.stop, P):
                nc.tensor.matmul(turned_ps[c][:, b - cols.start:b - cols.start + P], base_sb[:, b:b + P], ident[:],
                                 start=(b == cols.start), stop=False, is_transpose=True)
        tpb_th = pb_ground
        rest_banks = ("a_ps0", "a_ps1", "rest_ps2")
        rest_ps = []
        for c, cols in enumerate(PIECES):
            width = cols.stop - cols.start
            nc.gpsimd.tensor_tensor(tpb_th[:, cols], tpb[:, cols], th[:, cols], ALU.mult)
            for b in range(cols.start, cols.stop, P):
                nc.tensor.matmul(turned_ps[c][:, b - cols.start:b - cols.start + P], tpb_th[:, b:b + P], ident[:],
                                 start=False, stop=(b == cols.stop - P), is_transpose=True)
            turned = sb.tile([P, width], F32, name=f"turned{c}")
            nc.scalar.copy(out=turned[:], in_=turned_ps[c][:])
            rest_ps.append(psum.tile([P, width], F32, name=f"rest_ps{c}", tag=rest_banks[c]))
            for b in range(0, width, P):
                nc.tensor.transpose(rest_ps[c][:, b:b + P], turned[:, b:b + P], ident[:])

        lead = sb.tile([P, U], F32, name="lead")
        nc.vector.tensor_tensor(lead[:], tpa[:], coef[:], ALU.mult)
        for c, cols in enumerate(PIECES):
            res = sb.tile([P, cols.stop - cols.start], F32, name=f"res{c}")
            nc.vector.tensor_tensor(res[:], rest_ps[c][:], lead[:, cols], ALU.add)
            nc.sync.dma_start(out=out[:, cols], in_=res[:])
